import numpy as np
import ml_dtypes


def mxq(x, axis, fmt="e4m3"):
    dtype, down = {"e4m3": (ml_dtypes.float8_e4m3fn, 7), "e5m2": (ml_dtypes.float8_e5m2, 14)}[fmt]
    v = np.moveaxis(np.asarray(x, np.float32).astype(ml_dtypes.bfloat16).astype(np.float64), axis, -1)
    blocks = v.reshape(v.shape[:-1] + (-1, 32))
    amax = np.abs(blocks).max(-1, keepdims=True)
    byte = np.maximum(np.where(amax > 0, np.frexp(amax)[1] - 1 + 127, 0) - down, 1)
    scale = np.exp2(byte - 127.0)
    codes = (blocks / scale).astype(np.float32).astype(dtype).astype(np.float64)
    return np.moveaxis((codes * scale).reshape(v.shape), -1, axis)


WIDE = False


def mx_kscale(k):
    if not WIDE:
        return np.ones(k)
    levels = np.array([10, -10, 5, -5, 0])
    if k % 512:
        return np.exp2(np.random.permutation(np.resize(levels, k // 32))).repeat(32)
    a = np.empty((k // 512, 16))
    for p in range(k // 512):
        a[p, :8] = np.random.permutation(np.resize(levels, 8))
        for g in range(8):
            far = levels[np.abs(levels - a[p, g]) >= 10]
            a[p, g + 8] = far[np.random.randint(len(far))]
    return np.exp2(a.ravel()).repeat(32)


def f64(x):
    return np.asarray(x).astype(np.float64)


def striped(idx):
    return np.tile(idx.reshape(-1, 16).T, (8, 1)).astype(np.uint16)


def unstriped(offs):
    return offs[:16].T.reshape(-1).astype(np.int64)


def striped8(idx):
    return np.concatenate([x.reshape(-1, 16).T for x in idx]).astype(np.uint16)


def runs(offs, k):
    lists = np.stack([offs[16 * r : 16 * r + 16].T.reshape(-1) for r in range(8)]).astype(np.int64)
    return lists[np.arange(k) % 512 // 64]


def pack_weight(w):
    k, n = w.shape
    w = f64(np.asarray(w, np.float32).astype(ml_dtypes.bfloat16)).reshape(k // 32, 32, n)
    amax = np.abs(w).max(1)
    byte = np.clip(np.where(amax > 0, np.frexp(amax)[1] - 1 + 127 - 7, 1), 1, 254)
    scaled = (w * np.exp2(127.0 - byte)[:, None, :]).reshape(k, n).astype(np.float32)
    words = np.ascontiguousarray(scaled.reshape(k // 512, 128, 4, n).transpose(0, 1, 3, 2)).astype(ml_dtypes.float8_e4m3fn).view(np.uint8)
    return words, np.ascontiguousarray(byte.astype(np.uint8).reshape(k // 512, 16, n))


def unpack_weight(words, scales):
    g, p, n, _ = words.shape
    vals = np.ascontiguousarray(words).view(ml_dtypes.float8_e4m3fn).astype(np.float64) * np.repeat(np.exp2(scales.astype(np.float64) - 127.0), 8, axis=1)[..., None]
    return vals.transpose(0, 1, 3, 2).reshape(g * 512, n)


K, T, S, N, H, J, W = 512, 2048, 512, 512, 512, 512, 256


def setup_inputs():
    n = np.random.standard_normal
    s = mx_kscale(K)[:, None]
    u = mx_kscale(S)
    packed_xT = pack_weight(n((K, T)) * s)
    perm = np.stack([np.random.permutation(H) for _ in range(8)])
    return {
        "x_words": packed_xT[0],
        "x_scales": packed_xT[1],
        "wa": (n((K, H)) / np.sqrt(K) / s).astype(np.float32),
        "tab": n((S, J)).astype(np.float32),
        "gt": (np.random.uniform(0.5, 1.5, (S, 1)) * u[:, None]).astype(np.float32),
        "w1": (n((S, N)) / np.sqrt(S) / u[:, None]).astype(np.float32),
        "offs": striped(np.random.permutation(T)[:S]),
        "n1": striped8(np.random.randint(0, J, (8, H))),
        "n2": striped8(np.stack([np.random.permutation(H) for _ in range(8)])),
        "n3": striped8(perm[:, :W]),
        "n4": striped8(perm[:, W:]),
    }


def reference(x_words, x_scales, wa, tab, gt, w1, offs, n1, n2, n3, n4):
    xq = unpack_weight(x_words, x_scales)[:, unstriped(offs)]
    y = xq.T @ mxq(f64(wa), 0, "e4m3")
    z = f64(gt) * (np.abs(y - (y[np.arange(S)[:, None], runs(n2, S)]) - (f64(tab)[np.arange(S)[:, None], runs(n1, S)])))
    h = mxq(f64(w1), 0, "e4m3").T @ mxq(z, 0, "e4m3")
    pa = h[np.arange(N)[:, None], runs(n3, N)]
    pb = h[np.arange(N)[:, None], runs(n4, N)]
    ra = np.maximum(pa, pb)
    out = h.copy()
    out[np.arange(N)[:, None], runs(n3, N)] = ra
    return out

@@ -1,0 +1,209 @@
+from contextlib import ExitStack
+
+import concourse.mybir as mybir
+
+K, T, S, N, H, J, W = 512, 2048, 512, 512, 512, 512, 256
+FLOPS = 2 * K * S * H + 2 * S * N * H
+
+F32 = mybir.dt.float32
+BF16 = mybir.dt.bfloat16
+I32 = mybir.dt.int32
+U32 = mybir.dt.uint32
+U16 = mybir.dt.uint16
+U8 = mybir.dt.uint8
+FP8X4 = mybir.dt.float8_e4m3fn_x4
+ALU = mybir.AluOpType
+ACT = mybir.ActivationFunctionType
+
+P = 128
+PACK = 4
+HALF = H // 2
+PIECES = ((0, 256), (256, 384), (384, 512))
+
+
+def tile_picked_tokkinddfill_none_p_kernel(
+    tc, x_words, x_scales, wa, tab, gt, w1, offs, n1, n2, n3, n4, out
+):
+    nc = tc.nc
+    with ExitStack() as ctx:
+        keep = ctx.enter_context(tc.tile_pool(name="keep", bufs=1))
+        psum = ctx.enter_context(tc.psum_pool(name="psum", bufs=1))
+
+        def sb(name, shape, dtype):
+            return keep.tile(shape, dtype, name=name, align_bytes=64)
+
+        def entries(lst, lo, hi):
+            return lst[:, lo // 16 : hi // 16]
+
+        offs_sb = sb("offs_sb", [P, S // 16], U16)
+        n1_sb = sb("n1_sb", [P, H // 16], U16)
+        n2_sb = sb("n2_sb", [P, H // 16], U16)
+        n3_sb = sb("n3_sb", [P, W // 16], U16)
+        n4_sb = sb("n4_sb", [P, W // 16], U16)
+        xw = sb("xw", [P, T], U32)
+        xs = sb("xs", [P, T], U8)
+        xs_in = [sb("xs_in%d" % q, [P, T // 4], I32) for q in range(4)]
+        wa_raw = [sb("wa_raw%d" % a, [P, PACK, HALF], F32) for a in range(2)]
+        w1_raw = sb("w1_raw", [P, PACK, N], F32)
+        gt_sb = sb("gt_sb", [P, PACK], F32)
+        tabs = [sb("tab%d" % t, [P, J], F32) for t in range(PACK)]
+
+        for q in range(4):
+            queue = nc.scalar if q < 2 else nc.sync
+            queue.dma_start(out=xs_in[q][32 * q : 32 * q + 4, :], in_=x_scales[0, 4 * q : 4 * q + 4, :].bitcast(I32))
+        nc.sync.dma_start(offs_sb[:], offs)
+        nc.sync.dma_start(out=xw[:].bitcast(I32), in_=x_words[0].rearrange("p n t -> p (n t)").bitcast(I32))
+        wa_rows = wa.rearrange("(p j) c -> p j c", j=PACK)
+        for a in range(2):
+            nc.sync.dma_start(out=wa_raw[a][:], in_=wa_rows[:, :, a * HALF : (a + 1) * HALF])
+        nc.sync.dma_start(out=gt_sb[:], in_=gt.rearrange("(p t) o -> p (t o)", t=PACK))
+        nc.sync.dma_start(n1_sb[:], n1)
+        tab_rows = tab.rearrange("(p t) c -> p t c", t=PACK)
+        for t in range(PACK):
+            nc.sync.dma_start(out=tabs[t][:], in_=tab_rows[:, t, :])
+            if t == 0:
+                nc.sync.dma_start(n2_sb[:], n2)
+        nc.sync.dma_start(out=w1_raw[:], in_=w1.rearrange("(p j) c -> p j c", j=PACK))
+        nc.sync.dma_start(n3_sb[:], n3)
+        nc.sync.dma_start(n4_sb[:], n4)
+
+        nc.vector.memset(xs[:].bitcast(I32), 0)
+        for q in range(4):
+            nc.vector.tensor_copy(out=xs[32 * q : 32 * q + 4, :].bitcast(I32), in_=xs_in[q][32 * q : 32 * q + 4, :])
+        gw = sb("gw", [P, S], U32)
+        gs = sb("gs", [P, S], U8)
+        nc.vector.tensor_copy(out=gs[:].rearrange("p (t m) -> p m t", t=PACK), in_=xs[:].indirect(offs_sb[:]))
+        nc.vector.tensor_copy(out=gw[:].rearrange("p (t m) -> p m t", t=PACK), in_=xw[:].indirect(offs_sb[:]))
+
+        y_ps = [psum.tile([P, H], F32, name="y_ps%d" % t, tag="a%d" % t) for t in range(PACK)]
+        for a in range(2):
+            wa_bf = sb("wa_bf%d" % a, [P, HALF, PACK], BF16)
+            wa_codes = sb("wa_codes%d" % a, [P, HALF], U32)
+            wa_scales = sb("wa_scales%d" % a, [P, HALF], U8)
+            for copy, cols in ((nc.scalar.copy, slice(0, 96)), (nc.vector.tensor_copy, slice(96, HALF))):
+                copy(
+                    out=wa_bf[:, cols, :].rearrange("p (c i) j -> p c j i", i=4),
+                    in_=wa_raw[a][:, :, cols].rearrange("p j (c i) -> p c j i", i=4),
+                )
+            nc.vector.quantize_mx(
+                out=wa_codes[:].bitcast(FP8X4), scales=wa_scales[:], in_=wa_bf[:].rearrange("p c j -> p (c j)")
+            )
+            for t in range(PACK):
+                rows = slice(t * P, (t + 1) * P)
+                nc.tensor.matmul_mx(
+                    out=y_ps[t][:, a * HALF : (a + 1) * HALF],
+                    lhsT=gw[:, rows].bitcast(FP8X4),
+                    lhsT_scale=gs[:, rows],
+                    rhs=wa_codes[:].bitcast(FP8X4),
+                    rhs_scale=wa_scales[:],
+                    start=True,
+                    stop=True,
+                )
+
+        sign = sb("sign", [P, PACK], BF16)
+        nc.scalar.activation(out=sign[:], in_=gt_sb[:], func=ACT.Sign)
+
+        ys = [sb("y%d" % t, [P, H], F32) for t in range(PACK)]
+        kind = [sb("kind%d" % t, [P, H], F32) for t in range(PACK)]
+        part = [sb("part%d" % t, [P, H], F32) for t in range(PACK)]
+        diff = [sb("diff%d" % i, [P, PACK, hi - lo], F32) for i, (lo, hi) in enumerate(PIECES)]
+        z_abs = [sb("z_abs%d" % i, [P, hi - lo, PACK], BF16) for i, (lo, hi) in enumerate(PIECES)]
+        z_bf = [sb("z_bf%d" % i, [P, hi - lo, PACK], BF16) for i, (lo, hi) in enumerate(PIECES)]
+        z_codes = [sb("z_codes%d" % i, [P, hi - lo], U32) for i, (lo, hi) in enumerate(PIECES)]
+        z_scales = [sb("z_scales%d" % i, [P, hi - lo], U8) for i, (lo, hi) in enumerate(PIECES)]
+
+        def finish_diff(i, t):
+            lo, hi = PIECES[i]
+            nc.vector.tensor_tensor(
+                diff[i][:, t, :], ys[t][:].indirect(entries(n2_sb, lo, hi)), part[t][:, lo:hi], ALU.add
+            )
+
+        def size_of(i):
+            nc.scalar.activation(
+                out=z_abs[i][:].rearrange("p (c i) t -> p c t i", i=4),
+                in_=diff[i][:].rearrange("p t (c i) -> p c t i", i=4),
+                func=ACT.Abs,
+            )
+
+        def sign_z(i):
+            lo, hi = PIECES[i]
+            nc.vector.tensor_tensor(
+                z_bf[i][:], z_abs[i][:], sign[:].unsqueeze(1).to_broadcast([P, hi - lo, PACK]), ALU.mult
+            )
+
+        def quantise_z(i):
+            nc.vector.quantize_mx(
+                out=z_codes[i][:].bitcast(FP8X4), scales=z_scales[i][:], in_=z_bf[i][:].rearrange("p c t -> p (c t)")
+            )
+
+        for t in range(PACK):
+            gt_col = gt_sb[:, t : t + 1]
+            for a in range(2):
+                lo, hi = a * HALF, (a + 1) * HALF
+                nc.scalar.activation(out=kind[t][:, lo:hi], in_=tabs[t][:].indirect(entries(n1_sb, lo, hi)), func=ACT.Copy)
+            nc.scalar.activation(out=ys[t][:], in_=y_ps[t][:], func=ACT.Copy, scale=gt_col)
+            nc.vector.scalar_tensor_tensor(part[t][:], kind[t][:], gt_col, ys[t][:], ALU.mult, ALU.subtract)
+            finish_diff(0, t)
+
+        w1_codes = sb("w1_codes", [P, N], U32)
+        w1_scales = sb("w1_scales", [P, N], U8)
+        w1_bf = [sb("w1_bf%d" % u, [P, 2, P, PACK], BF16) for u in range(2)]
+        w1_view = w1_raw[:].rearrange("p j (m t) -> p m t j", t=PACK)
+        for u, copy in enumerate((nc.vector.tensor_copy, nc.scalar.copy)):
+            copy(out=w1_bf[u][:].rearrange("p t m j -> p m t j"), in_=w1_view[:, :, 2 * u : 2 * u + 2, :])
+
+        def quantise_w1(u):
+            cols = slice(u * 2 * P, (u + 1) * 2 * P)
+            nc.vector.quantize_mx(
+                out=w1_codes[:, cols].bitcast(FP8X4),
+                scales=w1_scales[:, cols],
+                in_=w1_bf[u][:].rearrange("p t m j -> p (t m j)"),
+            )
+
+        size_of(0)
+        for i in range(1, len(PIECES)):
+            for t in range(PACK):
+                finish_diff(i, t)
+            size_of(i)
+            sign_z(i - 1)
+            if i == 1:
+                quantise_w1(0)
+            quantise_z(i - 1)
+        quantise_w1(1)
+        sign_z(len(PIECES) - 1)
+        quantise_z(len(PIECES) - 1)
+
+        h_ps = [
+            [psum.tile([P, hi - lo], F32, name="h_ps%d_%d" % (i, t), tag="ba"[i % 2] + str(t)) for t in range(PACK)]
+            for i, (lo, hi) in enumerate(PIECES)
+        ]
+        hs = [sb("h%d" % t, [P, H], F32) for t in range(PACK)]
+
+        def second_product(i, t):
+            rows = slice(t * P, (t + 1) * P)
+            nc.tensor.matmul_mx(
+                out=h_ps[i][t][:],
+                lhsT=w1_codes[:, rows].bitcast(FP8X4),
+                lhsT_scale=w1_scales[:, rows],
+                rhs=z_codes[i][:].bitcast(FP8X4),
+                rhs_scale=z_scales[i][:],
+                start=True,
+                stop=True,
+            )
+
+        out_rows = out.rearrange("(p t) c -> p t c", t=PACK)
+        for t in range(PACK):
+            for i, (lo, hi) in enumerate(PIECES):
+                second_product(i, t)
+                nc.scalar.copy(out=hs[t][:, lo:hi], in_=h_ps[i][t][:])
+            pa = sb("pa%d" % t, [P, W], F32)
+            pb = sb("pb%d" % t, [P, W], F32)
+            ra = sb("ra%d" % t, [P, W], F32)
+            nc.scalar.activation(out=pa[:], in_=hs[t][:].indirect(n3_sb[:]), func=ACT.Copy)
+            if t == 0:
+                nc.vector.tensor_copy(out=pb[:], in_=hs[t][:].indirect(n4_sb[:]))
+            else:
+                nc.scalar.activation(out=pb[:], in_=hs[t][:].indirect(n4_sb[:]), func=ACT.Copy)
+            nc.vector.tensor_tensor(ra[:], pa[:], pb[:], ALU.max)
+            nc.vector.tensor_copy(out=hs[t][:].indirect(n3_sb[:]), in_=ra[:])
+            nc.sync.dma_start(out=out_rows[:, t, :], in_=hs[t][:])

@@ -18,6 +18,7 @@ ACT = mybir.ActivationFunctionType
 P = 128
 PACK = 4
 HALF = H // 2
+WA_SPLIT = (160, 96)
 PIECES = ((0, 256), (256, 384), (384, 512))
 
 
@@ -75,27 +76,30 @@ def tile_picked_tokkinddfill_none_p_kernel(
         nc.vector.tensor_copy(out=gs[:].rearrange("p (t m) -> p m t", t=PACK), in_=xs[:].indirect(offs_sb[:]))
         nc.vector.tensor_copy(out=gw[:].rearrange("p (t m) -> p m t", t=PACK), in_=xw[:].indirect(offs_sb[:]))
 
-        y_ps = [psum.tile([P, H], F32, name="y_ps%d" % t, tag="a%d" % t) for t in range(PACK)]
+        wa_codes = [sb("wa_codes%d" % a, [P, HALF], U32) for a in range(2)]
+        wa_scales = [sb("wa_scales%d" % a, [P, HALF], U8) for a in range(2)]
         for a in range(2):
             wa_bf = sb("wa_bf%d" % a, [P, HALF, PACK], BF16)
-            wa_codes = sb("wa_codes%d" % a, [P, HALF], U32)
-            wa_scales = sb("wa_scales%d" % a, [P, HALF], U8)
-            for copy, cols in ((nc.scalar.copy, slice(0, 96)), (nc.vector.tensor_copy, slice(96, HALF))):
+            for copy, cols in ((nc.scalar.copy, slice(0, WA_SPLIT[a])), (nc.vector.tensor_copy, slice(WA_SPLIT[a], HALF))):
                 copy(
                     out=wa_bf[:, cols, :].rearrange("p (c i) j -> p c j i", i=4),
                     in_=wa_raw[a][:, :, cols].rearrange("p j (c i) -> p c j i", i=4),
                 )
             nc.vector.quantize_mx(
-                out=wa_codes[:].bitcast(FP8X4), scales=wa_scales[:], in_=wa_bf[:].rearrange("p c j -> p (c j)")
+                out=wa_codes[a][:].bitcast(FP8X4), scales=wa_scales[a][:], in_=wa_bf[:].rearrange("p c j -> p (c j)")
             )
-            for t in range(PACK):
-                rows = slice(t * P, (t + 1) * P)
+
+        y0_ps = [psum.tile([P, HALF], F32, name="y0_ps%d" % a, tag="ba"[a] + "0") for a in range(2)]
+        y_ps = {t: psum.tile([P, H], F32, name="y_ps%d" % t, tag="a%d" % t) for t in range(1, PACK)}
+        for t in range(PACK):
+            rows = slice(t * P, (t + 1) * P)
+            for a in range(2):
                 nc.tensor.matmul_mx(
-                    out=y_ps[t][:, a * HALF : (a + 1) * HALF],
+                    out=y0_ps[a][:] if t == 0 else y_ps[t][:, a * HALF : (a + 1) * HALF],
                     lhsT=gw[:, rows].bitcast(FP8X4),
                     lhsT_scale=gs[:, rows],
-                    rhs=wa_codes[:].bitcast(FP8X4),
-                    rhs_scale=wa_scales[:],
+                    rhs=wa_codes[a][:].bitcast(FP8X4),
+                    rhs_scale=wa_scales[a][:],
                     start=True,
                     stop=True,
                 )
@@ -104,24 +108,55 @@ def tile_picked_tokkinddfill_none_p_kernel(
         nc.scalar.activation(out=sign[:], in_=gt_sb[:], func=ACT.Sign)
 
         ys = [sb("y%d" % t, [P, H], F32) for t in range(PACK)]
-        kind = [sb("kind%d" % t, [P, H], F32) for t in range(PACK)]
-        part = [sb("part%d" % t, [P, H], F32) for t in range(PACK)]
-        diff = [sb("diff%d" % i, [P, PACK, hi - lo], F32) for i, (lo, hi) in enumerate(PIECES)]
+        part = [[sb("part%d_%d" % (a, t), [P, HALF], F32) for t in range(PACK)] for a in range(2)]
+        diff = [sb("diff%d" % a, [P, PACK, HALF], F32) for a in range(2)]
         z_abs = [sb("z_abs%d" % i, [P, hi - lo, PACK], BF16) for i, (lo, hi) in enumerate(PIECES)]
         z_bf = [sb("z_bf%d" % i, [P, hi - lo, PACK], BF16) for i, (lo, hi) in enumerate(PIECES)]
-        z_codes = [sb("z_codes%d" % i, [P, hi - lo], U32) for i, (lo, hi) in enumerate(PIECES)]
-        z_scales = [sb("z_scales%d" % i, [P, hi - lo], U8) for i, (lo, hi) in enumerate(PIECES)]
+        z_codes = sb("z_codes", [P, H], U32)
+        z_scales = sb("z_scales", [P, H], U8)
+        kind = {}
 
-        def finish_diff(i, t):
-            lo, hi = PIECES[i]
+        def kind_tile(name, tag, count):
+            return keep.tile([P, count, HALF], F32, name=name, tag=tag, align_bytes=64)
+
+        def fetch_kind(a, t, on_vector, dst):
+            kind[a, t] = dst
+            window = tabs[t][:].indirect(entries(n1_sb, a * HALF, (a + 1) * HALF))
+            if on_vector:
+                nc.vector.tensor_copy(out=dst, in_=window)
+            else:
+                nc.scalar.activation(out=dst, in_=window, func=ACT.Copy)
+
+        def fetch_y(t):
+            if t == 0:
+                for a in range(2):
+                    nc.scalar.activation(
+                        out=ys[0][:, a * HALF : (a + 1) * HALF], in_=y0_ps[a][:], func=ACT.Copy, scale=gt_sb[:, 0:1]
+                    )
+            else:
+                nc.scalar.activation(out=ys[t][:], in_=y_ps[t][:], func=ACT.Copy, scale=gt_sb[:, t : t + 1])
+
+        def start_diff(a, t):
+            nc.vector.scalar_tensor_tensor(
+                part[a][t][:],
+                kind[a, t],
+                gt_sb[:, t : t + 1],
+                ys[t][:, a * HALF : (a + 1) * HALF],
+                ALU.mult,
+                ALU.subtract,
+            )
+
+        def finish_diff(a, t):
             nc.vector.tensor_tensor(
-                diff[i][:, t, :], ys[t][:].indirect(entries(n2_sb, lo, hi)), part[t][:, lo:hi], ALU.add
+                diff[a][:, t, :], ys[t][:].indirect(entries(n2_sb, a * HALF, (a + 1) * HALF)), part[a][t][:], ALU.add
             )
 
         def size_of(i):
+            lo, hi = PIECES[i]
+            a = lo // HALF
             nc.scalar.activation(
                 out=z_abs[i][:].rearrange("p (c i) t -> p c t i", i=4),
-                in_=diff[i][:].rearrange("p t (c i) -> p c t i", i=4),
+                in_=diff[a][:, :, lo - a * HALF : hi - a * HALF].rearrange("p t (c i) -> p c t i", i=4),
                 func=ACT.Abs,
             )
 
@@ -132,70 +167,76 @@ def tile_picked_tokkinddfill_none_p_kernel(
             )
 
         def quantise_z(i):
+            lo, hi = PIECES[i]
             nc.vector.quantize_mx(
-                out=z_codes[i][:].bitcast(FP8X4), scales=z_scales[i][:], in_=z_bf[i][:].rearrange("p c t -> p (c t)")
+                out=z_codes[:, lo:hi].bitcast(FP8X4),
+                scales=z_scales[:, lo:hi],
+                in_=z_bf[i][:].rearrange("p c t -> p (c t)"),
             )
 
+        early = kind_tile("kind_early", "wa_bf1", 2)
+        fetch_kind(0, 0, True, early[:, 0, :])
+        fetch_kind(0, 1, True, early[:, 1, :])
+        fetch_kind(1, 0, False, kind_tile("kind1_0", "kind0", 1)[:, 0, :])
         for t in range(PACK):
-            gt_col = gt_sb[:, t : t + 1]
-            for a in range(2):
-                lo, hi = a * HALF, (a + 1) * HALF
-                nc.scalar.activation(out=kind[t][:, lo:hi], in_=tabs[t][:].indirect(entries(n1_sb, lo, hi)), func=ACT.Copy)
-            nc.scalar.activation(out=ys[t][:], in_=y_ps[t][:], func=ACT.Copy, scale=gt_col)
-            nc.vector.scalar_tensor_tensor(part[t][:], kind[t][:], gt_col, ys[t][:], ALU.mult, ALU.subtract)
+            if t >= 2:
+                fetch_kind(0, t, False, kind_tile("kind0_%d" % t, "wa_codes%d" % (t - 2), 1)[:, 0, :])
+            fetch_y(t)
+            start_diff(0, t)
             finish_diff(0, t)
+        for t in range(PACK):
+            if t >= 1:
+                tag = "wa_bf1" if t == 1 else "wa_codes%d" % (t - 2)
+                fetch_kind(1, t, False, kind_tile("kind1_%d" % t, tag, 1)[:, 0, :])
+            start_diff(1, t)
+            finish_diff(1, t)
 
         w1_codes = sb("w1_codes", [P, N], U32)
         w1_scales = sb("w1_scales", [P, N], U8)
-        w1_bf = [sb("w1_bf%d" % u, [P, 2, P, PACK], BF16) for u in range(2)]
+        w1_bf = keep.tile([P, PACK, P, PACK], BF16, name="w1_bf", tag="tab3", align_bytes=64)
         w1_view = w1_raw[:].rearrange("p j (m t) -> p m t j", t=PACK)
-        for u, copy in enumerate((nc.vector.tensor_copy, nc.scalar.copy)):
-            copy(out=w1_bf[u][:].rearrange("p t m j -> p m t j"), in_=w1_view[:, :, 2 * u : 2 * u + 2, :])
+        w1_dst = w1_bf[:].rearrange("p t m j -> p m t j")
+        for lo, hi, copy in ((0, 64, nc.scalar.copy), (64, 128, nc.scalar.copy)):
+            copy(out=w1_dst[:, lo:hi], in_=w1_view[:, lo:hi])
 
-        def quantise_w1(u):
-            cols = slice(u * 2 * P, (u + 1) * 2 * P)
-            nc.vector.quantize_mx(
-                out=w1_codes[:, cols].bitcast(FP8X4),
-                scales=w1_scales[:, cols],
-                in_=w1_bf[u][:].rearrange("p t m j -> p (t m j)"),
-            )
-
-        size_of(0)
-        for i in range(1, len(PIECES)):
-            for t in range(PACK):
-                finish_diff(i, t)
+        nc.vector.quantize_mx(
+            out=w1_codes[:].bitcast(FP8X4), scales=w1_scales[:], in_=w1_bf[:].rearrange("p t m j -> p (t m j)")
+        )
+        for i in range(len(PIECES)):
             size_of(i)
-            sign_z(i - 1)
-            if i == 1:
-                quantise_w1(0)
-            quantise_z(i - 1)
-        quantise_w1(1)
-        sign_z(len(PIECES) - 1)
-        quantise_z(len(PIECES) - 1)
+            sign_z(i)
+            quantise_z(i)
 
-        h_ps = [
-            [psum.tile([P, hi - lo], F32, name="h_ps%d_%d" % (i, t), tag="ba"[i % 2] + str(t)) for t in range(PACK)]
-            for i, (lo, hi) in enumerate(PIECES)
-        ]
+        cut = PIECES[2][0]
         hs = [sb("h%d" % t, [P, H], F32) for t in range(PACK)]
 
-        def second_product(i, t):
+        def second_product(t, lo, hi, bank):
             rows = slice(t * P, (t + 1) * P)
             nc.tensor.matmul_mx(
-                out=h_ps[i][t][:],
+                out=bank,
                 lhsT=w1_codes[:, rows].bitcast(FP8X4),
                 lhsT_scale=w1_scales[:, rows],
-                rhs=z_codes[i][:].bitcast(FP8X4),
-                rhs_scale=z_scales[i][:],
+                rhs=z_codes[:, lo:hi].bitcast(FP8X4),
+                rhs_scale=z_scales[:, lo:hi],
                 start=True,
                 stop=True,
             )
 
         out_rows = out.rearrange("(p t) c -> p t c", t=PACK)
         for t in range(PACK):
-            for i, (lo, hi) in enumerate(PIECES):
-                second_product(i, t)
-                nc.scalar.copy(out=hs[t][:, lo:hi], in_=h_ps[i][t][:])
+            if t < 2:
+                h_first = psum.tile([P, cut], F32, name="h_first%d" % t, tag="b%d" % t)
+                h_last = psum.tile([P, H - cut], F32, name="h_last%d" % t, tag="a%d" % t)
+                for lo, hi in PIECES[:2]:
+                    second_product(t, lo, hi, h_first[:, lo:hi])
+                copy = nc.scalar.copy if t == 0 else nc.vector.tensor_copy
+                copy(out=hs[t][:, :cut], in_=h_first[:])
+                second_product(t, cut, H, h_last[:])
+                nc.scalar.copy(out=hs[t][:, cut:], in_=h_last[:])
+            else:
+                h_ps = psum.tile([P, H], F32, name="h_ps%d" % t, tag="a1")
+                second_product(t, 0, H, h_ps[:])
+                nc.scalar.copy(out=hs[t][:], in_=h_ps[:])
             pa = sb("pa%d" % t, [P, W], F32)
             pb = sb("pb%d" % t, [P, W], F32)
             ra = sb("ra%d" % t, [P, W], F32)

@@ -19,7 +19,7 @@ P = 128
 PACK = 4
 HALF = H // 2
 WA_SPLIT = (160, 96)
-PIECES = ((0, 256), (256, 384), (384, 512))
+PIECES = ((0, 256), (256, 512))
 
 
 def tile_picked_tokkinddfill_none_p_kernel(
@@ -76,8 +76,8 @@ def tile_picked_tokkinddfill_none_p_kernel(
         nc.vector.tensor_copy(out=gs[:].rearrange("p (t m) -> p m t", t=PACK), in_=xs[:].indirect(offs_sb[:]))
         nc.vector.tensor_copy(out=gw[:].rearrange("p (t m) -> p m t", t=PACK), in_=xw[:].indirect(offs_sb[:]))
 
-        wa_codes = [sb("wa_codes%d" % a, [P, HALF], U32) for a in range(2)]
-        wa_scales = [sb("wa_scales%d" % a, [P, HALF], U8) for a in range(2)]
+        wa_codes = sb("wa_codes", [P, H], U32)
+        wa_scales = sb("wa_scales", [P, H], U8)
         for a in range(2):
             wa_bf = sb("wa_bf%d" % a, [P, HALF, PACK], BF16)
             for copy, cols in ((nc.scalar.copy, slice(0, WA_SPLIT[a])), (nc.vector.tensor_copy, slice(WA_SPLIT[a], HALF))):
@@ -85,24 +85,29 @@ def tile_picked_tokkinddfill_none_p_kernel(
                     out=wa_bf[:, cols, :].rearrange("p (c i) j -> p c j i", i=4),
                     in_=wa_raw[a][:, :, cols].rearrange("p j (c i) -> p c j i", i=4),
                 )
+            half = slice(a * HALF, (a + 1) * HALF)
             nc.vector.quantize_mx(
-                out=wa_codes[a][:].bitcast(FP8X4), scales=wa_scales[a][:], in_=wa_bf[:].rearrange("p c j -> p (c j)")
+                out=wa_codes[:, half].bitcast(FP8X4), scales=wa_scales[:, half], in_=wa_bf[:].rearrange("p c j -> p (c j)")
+            )
+
+        def first_product(t, cols, bank):
+            rows = slice(t * P, (t + 1) * P)
+            nc.tensor.matmul_mx(
+                out=bank,
+                lhsT=gw[:, rows].bitcast(FP8X4),
+                lhsT_scale=gs[:, rows],
+                rhs=wa_codes[:, cols].bitcast(FP8X4),
+                rhs_scale=wa_scales[:, cols],
+                start=True,
+                stop=True,
             )
 
         y0_ps = [psum.tile([P, HALF], F32, name="y0_ps%d" % a, tag="ba"[a] + "0") for a in range(2)]
         y_ps = {t: psum.tile([P, H], F32, name="y_ps%d" % t, tag="a%d" % t) for t in range(1, PACK)}
-        for t in range(PACK):
-            rows = slice(t * P, (t + 1) * P)
-            for a in range(2):
-                nc.tensor.matmul_mx(
-                    out=y0_ps[a][:] if t == 0 else y_ps[t][:, a * HALF : (a + 1) * HALF],
-                    lhsT=gw[:, rows].bitcast(FP8X4),
-                    lhsT_scale=gs[:, rows],
-                    rhs=wa_codes[a][:].bitcast(FP8X4),
-                    rhs_scale=wa_scales[a][:],
-                    start=True,
-                    stop=True,
-                )
+        for a in range(2):
+            first_product(0, slice(a * HALF, (a + 1) * HALF), y0_ps[a][:])
+        for t in range(1, PACK):
+            first_product(t, slice(0, H), y_ps[t][:])
 
         sign = sb("sign", [P, PACK], BF16)
         nc.scalar.activation(out=sign[:], in_=gt_sb[:], func=ACT.Sign)
@@ -111,15 +116,13 @@ def tile_picked_tokkinddfill_none_p_kernel(
         part = [[sb("part%d_%d" % (a, t), [P, HALF], F32) for t in range(PACK)] for a in range(2)]
         diff = [sb("diff%d" % a, [P, PACK, HALF], F32) for a in range(2)]
         z_abs = [sb("z_abs%d" % i, [P, hi - lo, PACK], BF16) for i, (lo, hi) in enumerate(PIECES)]
-        z_bf = [sb("z_bf%d" % i, [P, hi - lo, PACK], BF16) for i, (lo, hi) in enumerate(PIECES)]
+        z_bf = {}
         z_codes = sb("z_codes", [P, H], U32)
         z_scales = sb("z_scales", [P, H], U8)
         kind = {}
 
-        def kind_tile(name, tag, count):
-            return keep.tile([P, count, HALF], F32, name=name, tag=tag, align_bytes=64)
-
-        def fetch_kind(a, t, on_vector, dst):
+        def fetch_kind(a, t, on_vector, tag):
+            dst = keep.tile([P, HALF], F32, name="kind%d_%d" % (a, t), tag=tag, align_bytes=64)[:]
             kind[a, t] = dst
             window = tabs[t][:].indirect(entries(n1_sb, a * HALF, (a + 1) * HALF))
             if on_vector:
@@ -162,6 +165,8 @@ def tile_picked_tokkinddfill_none_p_kernel(
 
         def sign_z(i):
             lo, hi = PIECES[i]
+            tag = "part1_3" if i == 0 else "z_bf%d" % i
+            z_bf[i] = keep.tile([P, hi - lo, PACK], BF16, name="z_bf%d" % i, tag=tag, align_bytes=64)
             nc.vector.tensor_tensor(
                 z_bf[i][:], z_abs[i][:], sign[:].unsqueeze(1).to_broadcast([P, hi - lo, PACK]), ALU.mult
             )
@@ -174,48 +179,63 @@ def tile_picked_tokkinddfill_none_p_kernel(
                 in_=z_bf[i][:].rearrange("p c t -> p (c t)"),
             )
 
-        early = kind_tile("kind_early", "wa_bf1", 2)
-        fetch_kind(0, 0, True, early[:, 0, :])
-        fetch_kind(0, 1, True, early[:, 1, :])
-        fetch_kind(1, 0, False, kind_tile("kind1_0", "kind0", 1)[:, 0, :])
+        slots = ("wa_bf1", "kind_odd")
+        fetch_kind(0, 0, True, slots[0])
+        fetch_kind(0, 1, True, slots[1])
+        fetch_kind(1, 0, False, "kind1_0")
         for t in range(PACK):
             if t >= 2:
-                fetch_kind(0, t, False, kind_tile("kind0_%d" % t, "wa_codes%d" % (t - 2), 1)[:, 0, :])
+                fetch_kind(0, t, False, slots[t % 2])
             fetch_y(t)
             start_diff(0, t)
             finish_diff(0, t)
         for t in range(PACK):
             if t >= 1:
-                tag = "wa_bf1" if t == 1 else "wa_codes%d" % (t - 2)
-                fetch_kind(1, t, False, kind_tile("kind1_%d" % t, tag, 1)[:, 0, :])
+                fetch_kind(1, t, False, slots[(t + 1) % 2])
             start_diff(1, t)
             finish_diff(1, t)
+        size_of(0)
 
-        w1_codes = sb("w1_codes", [P, N], U32)
-        w1_scales = sb("w1_scales", [P, N], U8)
-        w1_bf = keep.tile([P, PACK, P, PACK], BF16, name="w1_bf", tag="tab3", align_bytes=64)
-        w1_view = w1_raw[:].rearrange("p j (m t) -> p m t j", t=PACK)
-        w1_dst = w1_bf[:].rearrange("p t m j -> p m t j")
-        for lo, hi, copy in ((0, 64, nc.scalar.copy), (64, 128, nc.scalar.copy)):
-            copy(out=w1_dst[:, lo:hi], in_=w1_view[:, lo:hi])
+        w1_codes = {}
+        w1_scales = {}
+        w1_view = w1_raw[:].rearrange("p j (m t) -> p m j t", t=PACK)
+        w1_bf = {}
 
-        nc.vector.quantize_mx(
-            out=w1_codes[:].bitcast(FP8X4), scales=w1_scales[:], in_=w1_bf[:].rearrange("p t m j -> p (t m j)")
-        )
-        for i in range(len(PIECES)):
+        def round_w1(u, tag):
+            w1_bf[u] = keep.tile([P, 2, P, PACK], BF16, name="w1_bf%d" % u, tag=tag, align_bytes=64)
+            nc.scalar.copy(out=w1_bf[u][:].rearrange("p t m j -> p m j t"), in_=w1_view[:, :, :, 2 * u : 2 * u + 2])
+
+        def quantise_w1(u, tag):
+            w1_codes[u] = keep.tile([P, 2 * P], U32, name="w1_codes%d" % u, tag=tag, align_bytes=64)
+            w1_scales[u] = sb("w1_scales%d" % u, [P, 2 * P], U8)
+            nc.vector.quantize_mx(
+                out=w1_codes[u][:].bitcast(FP8X4),
+                scales=w1_scales[u][:],
+                in_=w1_bf[u][:].rearrange("p t m j -> p (t m j)"),
+            )
+
+        round_w1(0, "tab3")
+        sign_z(0)
+        quantise_w1(0, "w1_codes0")
+        quantise_z(0)
+        for i in range(1, len(PIECES)):
             size_of(i)
             sign_z(i)
             quantise_z(i)
+        round_w1(1, "diff1")
 
-        cut = PIECES[2][0]
-        hs = [sb("h%d" % t, [P, H], F32) for t in range(PACK)]
+        cut = PIECES[-1][0]
+        hs = [
+            keep.tile([P, H], F32, name="h%d" % t, tag="z_bf1" if t == 1 else "h%d" % t, align_bytes=64)
+            for t in range(PACK)
+        ]
 
         def second_product(t, lo, hi, bank):
-            rows = slice(t * P, (t + 1) * P)
+            rows = slice(t % 2 * P, (t % 2 + 1) * P)
             nc.tensor.matmul_mx(
                 out=bank,
-                lhsT=w1_codes[:, rows].bitcast(FP8X4),
-                lhsT_scale=w1_scales[:, rows],
+                lhsT=w1_codes[t // 2][:, rows].bitcast(FP8X4),
+                lhsT_scale=w1_scales[t // 2][:, rows],
                 rhs=z_codes[:, lo:hi].bitcast(FP8X4),
                 rhs_scale=z_scales[:, lo:hi],
                 start=True,
@@ -226,15 +246,15 @@ def tile_picked_tokkinddfill_none_p_kernel(
         for t in range(PACK):
             if t < 2:
                 h_first = psum.tile([P, cut], F32, name="h_first%d" % t, tag="b%d" % t)
-                h_last = psum.tile([P, H - cut], F32, name="h_last%d" % t, tag="a%d" % t)
-                for lo, hi in PIECES[:2]:
+                h_last = psum.tile([P, H - cut], F32, name="h_last%d" % t, tag="a0")
+                for lo, hi in PIECES[:-1]:
                     second_product(t, lo, hi, h_first[:, lo:hi])
                 copy = nc.scalar.copy if t == 0 else nc.vector.tensor_copy
                 copy(out=hs[t][:, :cut], in_=h_first[:])
                 second_product(t, cut, H, h_last[:])
                 nc.scalar.copy(out=hs[t][:, cut:], in_=h_last[:])
             else:
-                h_ps = psum.tile([P, H], F32, name="h_ps%d" % t, tag="a1")
+                h_ps = psum.tile([P, H], F32, name="h_ps%d" % t, tag="a0")
                 second_product(t, 0, H, h_ps[:])
                 nc.scalar.copy(out=hs[t][:], in_=h_ps[:])
             pa = sb("pa%d" % t, [P, W], F32)
@@ -246,5 +266,7 @@ def tile_picked_tokkinddfill_none_p_kernel(
             else:
                 nc.scalar.activation(out=pb[:], in_=hs[t][:].indirect(n4_sb[:]), func=ACT.Copy)
             nc.vector.tensor_tensor(ra[:], pa[:], pb[:], ALU.max)
+            if t == 0:
+                quantise_w1(1, "pb0")
             nc.vector.tensor_copy(out=hs[t][:].indirect(n3_sb[:]), in_=ra[:])
             nc.sync.dma_start(out=out_rows[:, t, :], in_=hs[t][:])

from contextlib import ExitStack

import concourse.mybir as mybir

K, T, S, N, H, J, W = 512, 2048, 512, 512, 512, 512, 256
FLOPS = 2 * K * S * H + 2 * S * N * H

F32 = mybir.dt.float32
BF16 = mybir.dt.bfloat16
I32 = mybir.dt.int32
U32 = mybir.dt.uint32
U16 = mybir.dt.uint16
U8 = mybir.dt.uint8
FP8X4 = mybir.dt.float8_e4m3fn_x4
ALU = mybir.AluOpType
ACT = mybir.ActivationFunctionType

P = 128
PACK = 4
HALF = H // 2
WA_SPLIT = (160, 96)
PIECES = ((0, 256), (256, 512))


def tile_picked_tokkinddfill_none_p_kernel(
    tc, x_words, x_scales, wa, tab, gt, w1, offs, n1, n2, n3, n4, out
):
    nc = tc.nc
    with ExitStack() as ctx:
        keep = ctx.enter_context(tc.tile_pool(name="keep", bufs=1))
        psum = ctx.enter_context(tc.psum_pool(name="psum", bufs=1))

        def sb(name, shape, dtype):
            return keep.tile(shape, dtype, name=name, align_bytes=64)

        def entries(lst, lo, hi):
            return lst[:, lo // 16 : hi // 16]

        offs_sb = sb("offs_sb", [P, S // 16], U16)
        n1_sb = sb("n1_sb", [P, H // 16], U16)
        n2_sb = sb("n2_sb", [P, H // 16], U16)
        n3_sb = sb("n3_sb", [P, W // 16], U16)
        n4_sb = sb("n4_sb", [P, W // 16], U16)
        xw = sb("xw", [P, T], U32)
        xs = sb("xs", [P, T], U8)
        xs_in = [sb("xs_in%d" % q, [P, T // 4], I32) for q in range(4)]
        wa_raw = [sb("wa_raw%d" % a, [P, PACK, HALF], F32) for a in range(2)]
        w1_raw = sb("w1_raw", [P, PACK, N], F32)
        gt_sb = sb("gt_sb", [P, PACK], F32)
        tabs = [sb("tab%d" % t, [P, J], F32) for t in range(PACK)]

        for q in range(4):
            queue = nc.scalar if q < 2 else nc.sync
            queue.dma_start(out=xs_in[q][32 * q : 32 * q + 4, :], in_=x_scales[0, 4 * q : 4 * q + 4, :].bitcast(I32))
        nc.sync.dma_start(offs_sb[:], offs)
        nc.sync.dma_start(out=xw[:].bitcast(I32), in_=x_words[0].rearrange("p n t -> p (n t)").bitcast(I32))
        wa_rows = wa.rearrange("(p j) c -> p j c", j=PACK)
        for a in range(2):
            nc.sync.dma_start(out=wa_raw[a][:], in_=wa_rows[:, :, a * HALF : (a + 1) * HALF])
        nc.sync.dma_start(out=gt_sb[:], in_=gt.rearrange("(p t) o -> p (t o)", t=PACK))
        nc.sync.dma_start(n1_sb[:], n1)
        tab_rows = tab.rearrange("(p t) c -> p t c", t=PACK)
        for t in range(PACK):
            nc.sync.dma_start(out=tabs[t][:], in_=tab_rows[:, t, :])
            if t == 0:
                nc.sync.dma_start(n2_sb[:], n2)
        nc.sync.dma_start(out=w1_raw[:], in_=w1.rearrange("(p j) c -> p j c", j=PACK))
        nc.sync.dma_start(n3_sb[:], n3)
        nc.sync.dma_start(n4_sb[:], n4)

        nc.vector.memset(xs[:].bitcast(I32), 0)
        for q in range(4):
            nc.vector.tensor_copy(out=xs[32 * q : 32 * q + 4, :].bitcast(I32), in_=xs_in[q][32 * q : 32 * q + 4, :])
        gw = sb("gw", [P, S], U32)
        gs = sb("gs", [P, S], U8)
        nc.vector.tensor_copy(out=gs[:].rearrange("p (t m) -> p m t", t=PACK), in_=xs[:].indirect(offs_sb[:]))
        nc.vector.tensor_copy(out=gw[:].rearrange("p (t m) -> p m t", t=PACK), in_=xw[:].indirect(offs_sb[:]))

        wa_codes = sb("wa_codes", [P, H], U32)
        wa_scales = sb("wa_scales", [P, H], U8)
        for a in range(2):
            wa_bf = sb("wa_bf%d" % a, [P, HALF, PACK], BF16)
            for copy, cols in ((nc.scalar.copy, slice(0, WA_SPLIT[a])), (nc.vector.tensor_copy, slice(WA_SPLIT[a], HALF))):
                copy(
                    out=wa_bf[:, cols, :].rearrange("p (c i) j -> p c j i", i=4),
                    in_=wa_raw[a][:, :, cols].rearrange("p j (c i) -> p c j i", i=4),
                )
            half = slice(a * HALF, (a + 1) * HALF)
            nc.vector.quantize_mx(
                out=wa_codes[:, half].bitcast(FP8X4), scales=wa_scales[:, half], in_=wa_bf[:].rearrange("p c j -> p (c j)")
            )

        def first_product(t, cols, bank):
            rows = slice(t * P, (t + 1) * P)
            nc.tensor.matmul_mx(
                out=bank,
                lhsT=gw[:, rows].bitcast(FP8X4),
                lhsT_scale=gs[:, rows],
                rhs=wa_codes[:, cols].bitcast(FP8X4),
                rhs_scale=wa_scales[:, cols],
                start=True,
                stop=True,
            )

        y0_ps = [psum.tile([P, HALF], F32, name="y0_ps%d" % a, tag="ba"[a] + "0") for a in range(2)]
        y_ps = {t: psum.tile([P, H], F32, name="y_ps%d" % t, tag="a%d" % t) for t in range(1, PACK)}
        for a in range(2):
            first_product(0, slice(a * HALF, (a + 1) * HALF), y0_ps[a][:])
        for t in range(1, PACK):
            first_product(t, slice(0, H), y_ps[t][:])

        sign = sb("sign", [P, PACK], BF16)
        nc.scalar.activation(out=sign[:], in_=gt_sb[:], func=ACT.Sign)

        ys = [sb("y%d" % t, [P, H], F32) for t in range(PACK)]
        part = [[sb("part%d_%d" % (a, t), [P, HALF], F32) for t in range(PACK)] for a in range(2)]
        diff = [sb("diff%d" % a, [P, PACK, HALF], F32) for a in range(2)]
        z_abs = [sb("z_abs%d" % i, [P, hi - lo, PACK], BF16) for i, (lo, hi) in enumerate(PIECES)]
        z_bf = {}
        z_codes = sb("z_codes", [P, H], U32)
        z_scales = sb("z_scales", [P, H], U8)
        kind = {}

        def fetch_kind(a, t, on_vector, tag):
            dst = keep.tile([P, HALF], F32, name="kind%d_%d" % (a, t), tag=tag, align_bytes=64)[:]
            kind[a, t] = dst
            window = tabs[t][:].indirect(entries(n1_sb, a * HALF, (a + 1) * HALF))
            if on_vector:
                nc.vector.tensor_copy(out=dst, in_=window)
            else:
                nc.scalar.activation(out=dst, in_=window, func=ACT.Copy)

        def fetch_y(t):
            if t == 0:
                for a in range(2):
                    nc.scalar.activation(
                        out=ys[0][:, a * HALF : (a + 1) * HALF], in_=y0_ps[a][:], func=ACT.Copy, scale=gt_sb[:, 0:1]
                    )
            else:
                nc.scalar.activation(out=ys[t][:], in_=y_ps[t][:], func=ACT.Copy, scale=gt_sb[:, t : t + 1])

        def start_diff(a, t):
            nc.vector.scalar_tensor_tensor(
                part[a][t][:],
                kind[a, t],
                gt_sb[:, t : t + 1],
                ys[t][:, a * HALF : (a + 1) * HALF],
                ALU.mult,
                ALU.subtract,
            )

        def finish_diff(a, t):
            nc.vector.tensor_tensor(
                diff[a][:, t, :], ys[t][:].indirect(entries(n2_sb, a * HALF, (a + 1) * HALF)), part[a][t][:], ALU.add
            )

        def size_of(i):
            lo, hi = PIECES[i]
            a = lo // HALF
            nc.scalar.activation(
                out=z_abs[i][:].rearrange("p (c i) t -> p c t i", i=4),
                in_=diff[a][:, :, lo - a * HALF : hi - a * HALF].rearrange("p t (c i) -> p c t i", i=4),
                func=ACT.Abs,
            )

        def sign_z(i):
            lo, hi = PIECES[i]
            tag = "part1_3" if i == 0 else "z_bf%d" % i
            z_bf[i] = keep.tile([P, hi - lo, PACK], BF16, name="z_bf%d" % i, tag=tag, align_bytes=64)
            nc.vector.tensor_tensor(
                z_bf[i][:], z_abs[i][:], sign[:].unsqueeze(1).to_broadcast([P, hi - lo, PACK]), ALU.mult
            )

        def quantise_z(i):
            lo, hi = PIECES[i]
            nc.vector.quantize_mx(
                out=z_codes[:, lo:hi].bitcast(FP8X4),
                scales=z_scales[:, lo:hi],
                in_=z_bf[i][:].rearrange("p c t -> p (c t)"),
            )

        slots = ("wa_bf1", "kind_odd")
        fetch_kind(0, 0, True, slots[0])
        fetch_kind(0, 1, True, slots[1])
        fetch_kind(1, 0, False, "kind1_0")
        for t in range(PACK):
            if t >= 2:
                fetch_kind(0, t, False, slots[t % 2])
            fetch_y(t)
            start_diff(0, t)
            finish_diff(0, t)
        for t in range(PACK):
            if t >= 1:
                fetch_kind(1, t, False, slots[(t + 1) % 2])
            start_diff(1, t)
            finish_diff(1, t)
        size_of(0)

        w1_codes = {}
        w1_scales = {}
        w1_view = w1_raw[:].rearrange("p j (m t) -> p m j t", t=PACK)
        w1_bf = {}

        def round_w1(u, tag):
            w1_bf[u] = keep.tile([P, 2, P, PACK], BF16, name="w1_bf%d" % u, tag=tag, align_bytes=64)
            nc.scalar.copy(out=w1_bf[u][:].rearrange("p t m j -> p m j t"), in_=w1_view[:, :, :, 2 * u : 2 * u + 2])

        def quantise_w1(u, tag):
            w1_codes[u] = keep.tile([P, 2 * P], U32, name="w1_codes%d" % u, tag=tag, align_bytes=64)
            w1_scales[u] = sb("w1_scales%d" % u, [P, 2 * P], U8)
            nc.vector.quantize_mx(
                out=w1_codes[u][:].bitcast(FP8X4),
                scales=w1_scales[u][:],
                in_=w1_bf[u][:].rearrange("p t m j -> p (t m j)"),
            )

        round_w1(0, "tab3")
        sign_z(0)
        quantise_w1(0, "w1_codes0")
        quantise_z(0)
        for i in range(1, len(PIECES)):
            size_of(i)
            sign_z(i)
            quantise_z(i)
        round_w1(1, "diff1")

        cut = PIECES[-1][0]
        hs = [
            keep.tile([P, H], F32, name="h%d" % t, tag="z_bf1" if t == 1 else "h%d" % t, align_bytes=64)
            for t in range(PACK)
        ]

        def second_product(t, lo, hi, bank):
            rows = slice(t % 2 * P, (t % 2 + 1) * P)
            nc.tensor.matmul_mx(
                out=bank,
                lhsT=w1_codes[t // 2][:, rows].bitcast(FP8X4),
                lhsT_scale=w1_scales[t // 2][:, rows],
                rhs=z_codes[:, lo:hi].bitcast(FP8X4),
                rhs_scale=z_scales[:, lo:hi],
                start=True,
                stop=True,
            )

        out_rows = out.rearrange("(p t) c -> p t c", t=PACK)
        for t in range(PACK):
            if t < 2:
                h_first = psum.tile([P, cut], F32, name="h_first%d" % t, tag="b%d" % t)
                h_last = psum.tile([P, H - cut], F32, name="h_last%d" % t, tag="a0")
                for lo, hi in PIECES[:-1]:
                    second_product(t, lo, hi, h_first[:, lo:hi])
                copy = nc.scalar.copy if t == 0 else nc.vector.tensor_copy
                copy(out=hs[t][:, :cut], in_=h_first[:])
                second_product(t, cut, H, h_last[:])
                nc.scalar.copy(out=hs[t][:, cut:], in_=h_last[:])
            else:
                h_ps = psum.tile([P, H], F32, name="h_ps%d" % t, tag="a0")
                second_product(t, 0, H, h_ps[:])
                nc.scalar.copy(out=hs[t][:], in_=h_ps[:])
            pa = sb("pa%d" % t, [P, W], F32)
            pb = sb("pb%d" % t, [P, W], F32)
            ra = sb("ra%d" % t, [P, W], F32)
            nc.scalar.activation(out=pa[:], in_=hs[t][:].indirect(n3_sb[:]), func=ACT.Copy)
            if t == 0:
                nc.vector.tensor_copy(out=pb[:], in_=hs[t][:].indirect(n4_sb[:]))
            else:
                nc.scalar.activation(out=pb[:], in_=hs[t][:].indirect(n4_sb[:]), func=ACT.Copy)
            nc.vector.tensor_tensor(ra[:], pa[:], pb[:], ALU.max)
            if t == 0:
                quantise_w1(1, "pb0")
            nc.vector.tensor_copy(out=hs[t][:].indirect(n3_sb[:]), in_=ra[:])
            nc.sync.dma_start(out=out_rows[:, t, :], in_=hs[t][:])
